import numpy as np
import ml_dtypes


def mxq(x, axis, fmt="e4m3"):
    dtype, down = {"e4m3": (ml_dtypes.float8_e4m3fn, 7), "e5m2": (ml_dtypes.float8_e5m2, 14)}[fmt]
    v = np.moveaxis(np.asarray(x, np.float32).astype(ml_dtypes.bfloat16).astype(np.float64), axis, -1)
    blocks = v.reshape(v.shape[:-1] + (-1, 32))
    amax = np.abs(blocks).max(-1, keepdims=True)
    byte = np.maximum(np.where(amax > 0, np.frexp(amax)[1] - 1 + 127, 0) - down, 1)
    scale = np.exp2(byte - 127.0)
    codes = (blocks / scale).astype(np.float32).astype(dtype).astype(np.float64)
    return np.moveaxis((codes * scale).reshape(v.shape), -1, axis)


WIDE = False


def mx_kscale(k):
    if not WIDE:
        return np.ones(k)
    levels = np.array([10, -10, 5, -5, 0])
    if k % 512:
        return np.exp2(np.random.permutation(np.resize(levels, k // 32))).repeat(32)
    a = np.empty((k // 512, 16))
    for p in range(k // 512):
        a[p, :8] = np.random.permutation(np.resize(levels, 8))
        for g in range(8):
            far = levels[np.abs(levels - a[p, g]) >= 10]
            a[p, g + 8] = far[np.random.randint(len(far))]
    return np.exp2(a.ravel()).repeat(32)


def f64(x):
    return np.asarray(x).astype(np.float64)


def striped(idx):
    return np.tile(idx.reshape(-1, 16).T, (8, 1)).astype(np.uint16)


def unstriped(offs):
    return offs[:16].T.reshape(-1).astype(np.int64)


def pack_weight(w):
    k, n = w.shape
    w = f64(np.asarray(w, np.float32).astype(ml_dtypes.bfloat16)).reshape(k // 32, 32, n)
    amax = np.abs(w).max(1)
    byte = np.clip(np.where(amax > 0, np.frexp(amax)[1] - 1 + 127 - 7, 1), 1, 254)
    scaled = (w * np.exp2(127.0 - byte)[:, None, :]).reshape(k, n).astype(np.float32)
    words = np.ascontiguousarray(scaled.reshape(k // 512, 128, 4, n).transpose(0, 1, 3, 2)).astype(ml_dtypes.float8_e4m3fn).view(np.uint8)
    return words, np.ascontiguousarray(byte.astype(np.uint8).reshape(k // 512, 16, n))


def unpack_weight(words, scales):
    g, p, n, _ = words.shape
    vals = np.ascontiguousarray(words).view(ml_dtypes.float8_e4m3fn).astype(np.float64) * np.repeat(np.exp2(scales.astype(np.float64) - 127.0), 8, axis=1)[..., None]
    return vals.transpose(0, 1, 3, 2).reshape(g * 512, n)


def gelu(v):
    return 0.5 * v * (1.0 + np.tanh(np.sqrt(2.0 / np.pi) * (v + 0.044715 * v**3)))


K, T, S, V, H, N = 1024, 1024, 512, 1024, 1024, 512
P = 2 ** 7


def setup_inputs():
    n = np.random.standard_normal
    s = mx_kscale(K)[:, None]
    u = mx_kscale(H)
    packed = pack_weight(n((K, T)) * s)
    return {
        "x_words": packed[0],
        "x_scales": packed[1],
        "w1": (n((K, H)) / np.sqrt(K) / s * u).astype(np.float32),
        "w2": (n((H, N)) / np.sqrt(H) / u[:, None]).astype(np.float32),
        "gate": np.tile(np.random.uniform(0.5, 1.5, S), (P, 1)).astype(np.float32),
        "offs": striped(np.random.permutation(T)[:S]),
        "pos1": striped(np.random.permutation(V)[:S]),
    }


def reference(x_words, x_scales, w1, w2, gate, offs, pos1):
    h = gelu(mxq(f64(w1), 0, "e4m3").T @ unpack_weight(x_words, x_scales)[:, unstriped(offs)])
    z = np.zeros((H, V))
    z[:, unstriped(pos1)] = f64(gate)[:1] * h
    return mxq(f64(w2), 0, "e4m3").T @ mxq(z, 0, "e4m3")

@@ -1,0 +1,304 @@
+from contextlib import ExitStack
+
+import concourse.mybir as mybir
+from concourse.masks import make_identity
+
+K, T, S, V, H, N = 1024, 1024, 512, 1024, 1024, 512
+FLOPS = 2 * K * H * S + 2 * H * N * V
+
+F32 = mybir.dt.float32
+BF16 = mybir.dt.bfloat16
+I32 = mybir.dt.int32
+U32 = mybir.dt.uint32
+U16 = mybir.dt.uint16
+U8 = mybir.dt.uint8
+FP8X4 = mybir.dt.float8_e4m3fn_x4
+MULT = mybir.AluOpType.mult
+GELU = mybir.ActivationFunctionType.Gelu_apprx_tanh
+
+P = 128
+PACK = 4
+KP = P * PACK
+BANK = 512
+WINDOWS = 4
+
+
+def tile_picked_voxel_gelu_p_kernel(
+    tc, x_words, x_scales, w1, w2, gate, offs, pos1, out
+):
+    nc = tc.nc
+    with ExitStack() as ctx:
+        lists = ctx.enter_context(tc.tile_pool(name="lists", bufs=1))
+        keep = ctx.enter_context(tc.tile_pool(name="keep", bufs=1))
+        psum = ctx.enter_context(tc.psum_pool(name="psum", bufs=1))
+
+        def sb(name, shape, dtype, tag=None):
+            return keep.tile(shape, dtype, name=name, tag=tag or name, align_bytes=64)
+
+        def bank(b, shape):
+            return psum.tile(shape, F32, name="bank%d" % b)
+
+        offs_sb = lists.tile([P, S // 16], U16, name="offs_sb")
+        pos_sb = lists.tile([P, S // 16], U16, name="pos_sb")
+        xs_all = sb("xs_all", [P, T // 4], I32)
+        xw_all = [sb("xw_all%d" % g, [P, T], I32) for g in range(2)]
+        xs = sb("xs", [P, S], U8)
+        xw = [sb("xw%d" % g, [P, S], U32) for g in range(2)]
+        gate_sb = sb("gate_sb", [P, S], F32)
+        windows = [sb("window%d" % i, [P, V], F32) for i in range(WINDOWS)]
+        ident = sb("ident", [P, P], F32)
+        warm = sb("warm", [P, 8], F32)
+
+        pieces = [(0, 128), (128, 128), (256, 128), (384, 128), (512, 256), (768, 256)]
+        raw1 = {}
+        for c0, wd in pieces:
+            for g in range(2):
+                raw1[c0, g] = sb("raw1_%d_%d" % (c0, g), [P, PACK, wd], F32)
+        raw2 = {(g, u): sb("raw2_%d_%d" % (g, u), [P, PACK, 256], F32) for g in range(2) for u in range(2)}
+
+        def load_w1(c0, wd, g):
+            rows = w1[g * KP : (g + 1) * KP, c0 : c0 + wd]
+            nc.sync.dma_start(out=raw1[c0, g][:], in_=rows.rearrange("(p j) c -> p j c", j=PACK))
+
+        def load_x(g):
+            nc.sync.dma_start(out=xw_all[g][:], in_=x_words[g].rearrange("p c r -> p (c r)").bitcast(I32))
+
+        nc.vector.memset(xs_all[:], 0)
+        nc.vector.memset(warm[:], 0.0)
+        nc.scalar.activation(out=warm[:, 4:5], in_=warm[:, 0:1], func=GELU)
+        nc.sync.dma_start(offs_sb[:], offs)
+        for q in range(4):
+            nc.sync.dma_start(
+                out=xs_all[32 * q : 32 * q + 8, :], in_=x_scales[:, 4 * q : 4 * q + 4, :].bitcast(I32)
+            )
+        load_x(0)
+        load_w1(0, 128, 0)
+        load_w1(0, 128, 1)
+        load_x(1)
+        nc.sync.dma_start(out=gate_sb[:], in_=gate)
+        nc.sync.dma_start(pos_sb[:], pos1)
+        for c0, wd in pieces[1:4]:
+            for g in range(2):
+                load_w1(c0, wd, g)
+        for g in range(2):
+            for c0, wd in pieces[4:]:
+                load_w1(c0, wd, g)
+        for g in range(2):
+            for u in range(2):
+                rows = w2[g * KP : (g + 1) * KP, 256 * u : 256 * (u + 1)]
+                nc.sync.dma_start(out=raw2[g, u][:], in_=rows.rearrange("(p j) n -> p j n", j=PACK))
+        nc.vector.memset(windows[0][:], 0.0)
+        for win in windows[1:]:
+            nc.gpsimd.memset(win[:], 0.0)
+        make_identity(nc, ident[:])
+
+        def interleave(dst, src):
+            nc.scalar.copy(
+                out=dst.rearrange("p (c i) j -> p c j i", i=4), in_=src.rearrange("p j (c i) -> p c j i", i=4)
+            )
+
+        def quantize(codes, scales, grouped):
+            nc.vector.quantize_mx(out=codes.bitcast(FP8X4), scales=scales, in_=grouped)
+
+        g1a = [sb("g1a_%d" % c, [P, 2, P, PACK], BF16) for c in range(4)]
+        c1a = [sb("c1a_%d" % c, [P, 2, P], U32) for c in range(4)]
+        s1a = [sb("s1a_%d" % c, [P, 2, P], U8) for c in range(4)]
+        g1b = [sb("g1b_%d" % g, [P, PACK, P, PACK], BF16) for g in range(2)]
+        c1b = [sb("c1b_%d" % g, [P, PACK, P], U32) for g in range(2)]
+        s1b = [sb("s1b_%d" % g, [P, PACK, P], U8) for g in range(2)]
+        g2 = [sb("g2_%d" % g, [P, N, PACK], BF16) for g in range(2)]
+        c2 = [sb("c2_%d" % g, [P, N], U32) for g in range(2)]
+        s2 = [sb("s2_%d" % g, [P, N], U8) for g in range(2)]
+        h = {}
+        gz = [sb("gz%d" % g, [P, V, PACK], BF16) for g in range(2)]
+        cz = [sb("cz%d" % g, [P, V], U32) for g in range(2)]
+        sz = [sb("sz%d" % g, [P, V], U8) for g in range(2)]
+        res = [sb("res%d" % i, [P, BANK], F32) for i in range(8)]
+
+        def cast_a(c, g):
+            interleave(g1a[c][:, g, :, :], raw1[c * P, g][:])
+
+        def quant_a(c):
+            quantize(
+                c1a[c][:].rearrange("p g m -> p (g m)"),
+                s1a[c][:].rearrange("p g m -> p (g m)"),
+                g1a[c][:].rearrange("p g m j -> p (g m j)"),
+            )
+
+        def cast_b(g, half):
+            nc.scalar.copy(
+                out=g1b[g][:, :, 64 * half : 64 * half + 64, :].rearrange("p t m j -> p m j t"),
+                in_=raw1[512 + 256 * half, g][:].rearrange("p j (m t) -> p m j t", t=PACK),
+            )
+
+        def quant_b(g):
+            quantize(
+                c1b[g][:].rearrange("p t m -> p (t m)"),
+                s1b[g][:].rearrange("p t m -> p (t m)"),
+                g1b[g][:].rearrange("p t m j -> p (t m j)"),
+            )
+
+        def layer1(i, b, lo, hi, tag=None):
+            acc = bank(b, [P, hi - lo])
+            for g in range(2):
+                if i < 4:
+                    codes, scales = c1a[i][:, g, :], s1a[i][:, g, :]
+                else:
+                    codes, scales = c1b[g][:, i - 4, :], s1b[g][:, i - 4, :]
+                nc.tensor.matmul_mx(
+                    out=acc[:],
+                    lhsT=codes.bitcast(FP8X4),
+                    lhsT_scale=scales,
+                    rhs=xw[g][:, lo:hi].bitcast(FP8X4),
+                    rhs_scale=xs[4 * g :, lo:hi],
+                    start=(g == 0),
+                    stop=(g == 1),
+                )
+            h[i, hi] = sb("h%d_%d" % (i, lo), [P, hi - lo], F32, tag)
+            nc.scalar.activation(out=h[i, hi][:], in_=acc[:], func=GELU)
+
+        def scatter(i, lo, hi):
+            nc.vector.tensor_tensor(
+                windows[i % WINDOWS][:].indirect(pos_sb[:, lo // 16 : hi // 16]),
+                h[i, hi][:],
+                gate_sb[:, lo:hi],
+                MULT,
+            )
+
+        turned = {}
+
+        def turn(i):
+            for half in range(2):
+                t = bank(2 + (2 * i + half) % 6, [P, 4, P])
+                for b in range(4):
+                    v0 = (4 * half + b) * P
+                    nc.tensor.transpose(t[:, b, :], windows[i % WINDOWS][:, v0 : v0 + P], ident[:])
+                turned[i, half] = t
+
+        def round_turned(i):
+            for half in range(2):
+                nc.scalar.copy(out=zt[:, 4 * half : 4 * half + 4, i * P : (i + 1) * P], in_=turned[i, half][:])
+
+        def turn_back(q):
+            t = bank(4 + q, [P, 2, 2, P])
+            for b in range(2):
+                words = zt[:, 2 * q + b, :].bitcast(F32)
+                for u in range(2):
+                    nc.tensor.transpose(t[:, b, u, :], words[:, u : 2 * P : 2], ident[:])
+            dst = gz[0][:, 256 * q : 256 * (q + 1), :].rearrange("p v j -> p (v j)").bitcast(F32)
+            nc.scalar.copy(
+                out=dst.rearrange("p (b v u) -> p b v u", b=2, u=2), in_=t[:].rearrange("p b u v -> p b v u")
+            )
+
+        def round_pair(i, lo, hi):
+            t = i - 4
+            nc.scalar.copy(out=pairs[:, t // 2, lo:hi, t % 2], in_=windows[i % WINDOWS][:, lo:hi])
+
+        def join_pairs(lo, hi):
+            src = pairs[:].rearrange("p u v e -> p u (v e)").bitcast(F32)
+            dst = gz[1][:, lo:hi, :].rearrange("p v j -> p (v j)").bitcast(F32)
+            nc.vector.tensor_copy(
+                out=dst.rearrange("p (v u) -> p v u", u=2), in_=src[:, :, lo:hi].rearrange("p u v -> p v u")
+            )
+
+        def cast_w2(g, u):
+            interleave(g2[g][:, 256 * u : 256 * (u + 1), :], raw2[g, u][:])
+
+        def quant_z(g, lo, hi):
+            quantize(cz[g][:, lo:hi], sz[g][:, lo:hi], gz[g][:, lo:hi, :].rearrange("p v j -> p (v j)"))
+
+        accs = {}
+
+        def layer2(g, half):
+            for m in range(4):
+                if g == 0:
+                    accs[half, m] = bank(4 * half + m, [P, BANK])
+                cols = slice(half * BANK, (half + 1) * BANK)
+                nc.tensor.matmul_mx(
+                    out=accs[half, m][:],
+                    lhsT=c2[g][:, m * P : (m + 1) * P].bitcast(FP8X4),
+                    lhsT_scale=s2[g][:, m * P : (m + 1) * P],
+                    rhs=cz[g][:, cols].bitcast(FP8X4),
+                    rhs_scale=sz[g][:, cols],
+                    start=(g == 0),
+                    stop=(g == 1),
+                )
+
+        def gather_words(g, lo, hi):
+            nc.vector.tensor_copy(
+                xw[g][:, lo:hi], xw_all[g][:].bitcast(U32).indirect(offs_sb[:, lo // 16 : hi // 16])
+            )
+
+        nc.vector.tensor_copy(xs[:], xs_all[:].bitcast(U8).indirect(offs_sb[:]))
+        gather_words(0, 0, S)
+        for g in range(2):
+            cast_a(0, g)
+            quantize(c1a[0][:, g, :], s1a[0][:, g, :], g1a[0][:, g, :, :].rearrange("p m j -> p (m j)"))
+        gather_words(1, 0, 256)
+        gather_words(1, 256, S)
+        layer1(0, 0, 0, 256)
+        scatter(0, 0, 256)
+        cast_a(1, 0)
+        cast_a(1, 1)
+        quant_a(1)
+        layer1(0, 1, 256, S, "raw1_128_1")
+        scatter(0, 256, S)
+        for c in range(2, 4):
+            cast_a(c, 0)
+            cast_a(c, 1)
+            quant_a(c)
+            layer1(c - 1, c % 2, 0, S, "raw1_%d_1" % (c * P))
+            turn(c - 2)
+            scatter(c - 1, 0, S)
+        for g in range(2):
+            cast_b(g, 0)
+            cast_b(g, 1)
+            quant_b(g)
+        layer1(3, 0, 0, S, "raw1_768_1")
+        turn(2)
+        scatter(3, 0, S)
+        zt = sb("zt", [P, 8, KP], BF16, "raw1_512_1")
+        layer1(4, 1, 0, S)
+        round_turned(0)
+        round_turned(1)
+        layer1(5, 0, 0, S)
+        round_turned(2)
+        turn(3)
+        scatter(4, 0, S)
+        scatter(5, 0, S)
+        cast_w2(0, 0)
+        cast_w2(0, 1)
+        pairs = sb("pairs", [P, 2, V, 2], BF16, "raw2_0_0")
+        round_turned(3)
+        layer1(6, 1, 0, S)
+        round_pair(4, 0, V)
+        scatter(6, 0, S)
+        cast_w2(1, 0)
+        cast_w2(1, 1)
+        for g in range(2):
+            quantize(c2[g][:], s2[g][:], g2[g][:].rearrange("p n j -> p (n j)"))
+        for q in range(4):
+            turn_back(q)
+        quant_z(0, 0, V)
+        layer1(7, 5, 0, S)
+        scatter(7, 0, S)
+        round_pair(5, 0, V)
+        round_pair(6, 0, V)
+        layer2(0, 0)
+        layer2(0, 1)
+        for q in range(4):
+            round_pair(7, 256 * q, 256 * (q + 1))
+        for half in range(2):
+            for q in (2 * half, 2 * half + 1):
+                join_pairs(256 * q, 256 * (q + 1))
+            for q in (2 * half, 2 * half + 1):
+                quant_z(1, 256 * q, 256 * (q + 1))
+            layer2(1, half)
+        for half in range(2):
+            for m in range(4):
+                i = 4 * half + m
+                if i in (2, 4, 6):
+                    nc.vector.tensor_copy(out=res[i][:], in_=accs[half, m][:])
+                else:
+                    nc.scalar.copy(out=res[i][:], in_=accs[half, m][:])
+                nc.sync.dma_start(out=out[m * P : (m + 1) * P, half * BANK : (half + 1) * BANK], in_=res[i][:])

@@ -20,7 +20,8 @@ P = 128
 PACK = 4
 KP = P * PACK
 BANK = 512
-WINDOWS = 4
+WINDOWS = 3
+SLOT = {4: 2, 5: 0, 6: 1, 7: 3}
 
 
 def tile_picked_voxel_gelu_p_kernel(
@@ -49,12 +50,12 @@ def tile_picked_voxel_gelu_p_kernel(
         ident = sb("ident", [P, P], F32)
         warm = sb("warm", [P, 8], F32)
 
-        pieces = [(0, 128), (128, 128), (256, 128), (384, 128), (512, 256), (768, 256)]
+        pieces = [(0, 128), (128, 128), (256, 128), (384, 128), (512, 512)]
         raw1 = {}
         for c0, wd in pieces:
             for g in range(2):
                 raw1[c0, g] = sb("raw1_%d_%d" % (c0, g), [P, PACK, wd], F32)
-        raw2 = {(g, u): sb("raw2_%d_%d" % (g, u), [P, PACK, 256], F32) for g in range(2) for u in range(2)}
+        raw2 = [sb("raw2_%d" % g, [P, PACK, N], F32) for g in range(2)]
 
         def load_w1(c0, wd, g):
             rows = w1[g * KP : (g + 1) * KP, c0 : c0 + wd]
@@ -63,20 +64,20 @@ def tile_picked_voxel_gelu_p_kernel(
         def load_x(g):
             nc.sync.dma_start(out=xw_all[g][:], in_=x_words[g].rearrange("p c r -> p (c r)").bitcast(I32))
 
-        nc.vector.memset(xs_all[:], 0)
-        nc.vector.memset(warm[:], 0.0)
+        nc.gpsimd.memset(xs_all[:], 0)
+        nc.gpsimd.memset(warm[:], 0.0)
         nc.scalar.activation(out=warm[:, 4:5], in_=warm[:, 0:1], func=GELU)
         nc.sync.dma_start(offs_sb[:], offs)
+        load_x(0)
         for q in range(4):
             nc.sync.dma_start(
                 out=xs_all[32 * q : 32 * q + 8, :], in_=x_scales[:, 4 * q : 4 * q + 4, :].bitcast(I32)
             )
-        load_x(0)
         load_w1(0, 128, 0)
         load_w1(0, 128, 1)
         load_x(1)
-        nc.sync.dma_start(out=gate_sb[:], in_=gate)
         nc.sync.dma_start(pos_sb[:], pos1)
+        nc.sync.dma_start(out=gate_sb[:], in_=gate)
         for c0, wd in pieces[1:4]:
             for g in range(2):
                 load_w1(c0, wd, g)
@@ -84,16 +85,15 @@ def tile_picked_voxel_gelu_p_kernel(
             for c0, wd in pieces[4:]:
                 load_w1(c0, wd, g)
         for g in range(2):
-            for u in range(2):
-                rows = w2[g * KP : (g + 1) * KP, 256 * u : 256 * (u + 1)]
-                nc.sync.dma_start(out=raw2[g, u][:], in_=rows.rearrange("(p j) n -> p j n", j=PACK))
+            rows = w2[g * KP : (g + 1) * KP, :]
+            nc.sync.dma_start(out=raw2[g][:], in_=rows.rearrange("(p j) n -> p j n", j=PACK))
         nc.vector.memset(windows[0][:], 0.0)
         for win in windows[1:]:
             nc.gpsimd.memset(win[:], 0.0)
         make_identity(nc, ident[:])
 
-        def interleave(dst, src):
-            nc.scalar.copy(
+        def interleave(dst, src, copy=nc.scalar.copy):
+            copy(
                 out=dst.rearrange("p (c i) j -> p c j i", i=4), in_=src.rearrange("p j (c i) -> p c j i", i=4)
             )
 
@@ -128,7 +128,7 @@ def tile_picked_voxel_gelu_p_kernel(
         def cast_b(g, half):
             nc.scalar.copy(
                 out=g1b[g][:, :, 64 * half : 64 * half + 64, :].rearrange("p t m j -> p m j t"),
-                in_=raw1[512 + 256 * half, g][:].rearrange("p j (m t) -> p m j t", t=PACK),
+                in_=raw1[512, g][:, :, 256 * half : 256 * (half + 1)].rearrange("p j (m t) -> p m j t", t=PACK),
             )
 
         def quant_b(g):
@@ -144,7 +144,7 @@ def tile_picked_voxel_gelu_p_kernel(
                 if i < 4:
                     codes, scales = c1a[i][:, g, :], s1a[i][:, g, :]
                 else:
-                    codes, scales = c1b[g][:, i - 4, :], s1b[g][:, i - 4, :]
+                    codes, scales = c1b[g][:, SLOT[i], :], s1b[g][:, SLOT[i], :]
                 nc.tensor.matmul_mx(
                     out=acc[:],
                     lhsT=codes.bitcast(FP8X4),
@@ -167,9 +167,9 @@ def tile_picked_voxel_gelu_p_kernel(
 
         turned = {}
 
-        def turn(i):
-            for half in range(2):
-                t = bank(2 + (2 * i + half) % 6, [P, 4, P])
+        def turn(i, halves=(0, 1)):
+            for half in halves:
+                t = bank((2 + 2 * (i % 3)) % 6 + half, [P, 4, P])
                 for b in range(4):
                     v0 = (4 * half + b) * P
                     nc.tensor.transpose(t[:, b, :], windows[i % WINDOWS][:, v0 : v0 + P], ident[:])
@@ -190,9 +190,9 @@ def tile_picked_voxel_gelu_p_kernel(
                 out=dst.rearrange("p (b v u) -> p b v u", b=2, u=2), in_=t[:].rearrange("p b u v -> p b v u")
             )
 
-        def round_pair(i, lo, hi):
-            t = i - 4
-            nc.scalar.copy(out=pairs[:, t // 2, lo:hi, t % 2], in_=windows[i % WINDOWS][:, lo:hi])
+        def round_pair(i, lo, hi, copy=nc.scalar.copy):
+            t = SLOT[i]
+            copy(out=pairs[:, t // 2, lo:hi, t % 2], in_=windows[i % WINDOWS][:, lo:hi])
 
         def join_pairs(lo, hi):
             src = pairs[:].rearrange("p u v e -> p u (v e)").bitcast(F32)
@@ -201,8 +201,8 @@ def tile_picked_voxel_gelu_p_kernel(
                 out=dst.rearrange("p (v u) -> p v u", u=2), in_=src[:, :, lo:hi].rearrange("p u v -> p v u")
             )
 
-        def cast_w2(g, u):
-            interleave(g2[g][:, 256 * u : 256 * (u + 1), :], raw2[g, u][:])
+        def cast_w2(g, u, copy=nc.scalar.copy):
+            interleave(g2[g][:, 256 * u : 256 * (u + 1), :], raw2[g][:, :, 256 * u : 256 * (u + 1)], copy)
 
         def quant_z(g, lo, hi):
             quantize(cz[g][:, lo:hi], sz[g][:, lo:hi], gz[g][:, lo:hi, :].rearrange("p v j -> p (v j)"))
@@ -229,8 +229,8 @@ def tile_picked_voxel_gelu_p_kernel(
                 xw[g][:, lo:hi], xw_all[g][:].bitcast(U32).indirect(offs_sb[:, lo // 16 : hi // 16])
             )
 
-        nc.vector.tensor_copy(xs[:], xs_all[:].bitcast(U8).indirect(offs_sb[:]))
         gather_words(0, 0, S)
+        nc.vector.tensor_copy(xs[:], xs_all[:].bitcast(U8).indirect(offs_sb[:]))
         for g in range(2):
             cast_a(0, g)
             quantize(c1a[0][:, g, :], s1a[0][:, g, :], g1a[0][:, g, :, :].rearrange("p m j -> p (m j)"))
@@ -254,41 +254,43 @@ def tile_picked_voxel_gelu_p_kernel(
             cast_b(g, 0)
             cast_b(g, 1)
             quant_b(g)
-        layer1(3, 0, 0, S, "raw1_768_1")
-        turn(2)
+        layer1(3, 0, 0, S, "raw1_512_1")
+        turn(2, (0,))
         scatter(3, 0, S)
-        zt = sb("zt", [P, 8, KP], BF16, "raw1_512_1")
+        zt = sb("zt", [P, 8, KP], BF16, "g1b_1")
         layer1(4, 1, 0, S)
+        turn(2, (1,))
         round_turned(0)
         round_turned(1)
-        layer1(5, 0, 0, S)
+        layer1(5, 6, 0, S)
         round_turned(2)
         turn(3)
         scatter(4, 0, S)
         scatter(5, 0, S)
         cast_w2(0, 0)
         cast_w2(0, 1)
-        pairs = sb("pairs", [P, 2, V, 2], BF16, "raw2_0_0")
+        pairs = sb("pairs", [P, 2, V, 2], BF16, "raw2_0")
         round_turned(3)
-        layer1(6, 1, 0, S)
+        layer1(6, 7, 0, S)
         round_pair(4, 0, V)
         scatter(6, 0, S)
         cast_w2(1, 0)
         cast_w2(1, 1)
         for g in range(2):
             quantize(c2[g][:], s2[g][:], g2[g][:].rearrange("p n j -> p (n j)"))
-        for q in range(4):
-            turn_back(q)
-        quant_z(0, 0, V)
-        layer1(7, 5, 0, S)
-        scatter(7, 0, S)
+        for half in range(2):
+            turn_back(2 * half)
+            turn_back(2 * half + 1)
+            quant_z(0, half * BANK, (half + 1) * BANK)
+            layer1(7, 4 + 2 * half, 256 * half, 256 * (half + 1))
+            scatter(7, 256 * half, 256 * (half + 1))
         round_pair(5, 0, V)
         round_pair(6, 0, V)
         layer2(0, 0)
         layer2(0, 1)
-        for q in range(4):
-            round_pair(7, 256 * q, 256 * (q + 1))
         for half in range(2):
+            for q in (2 * half, 2 * half + 1):
+                round_pair(7, 256 * q, 256 * (q + 1), nc.vector.tensor_copy)
             for q in (2 * half, 2 * half + 1):
                 join_pairs(256 * q, 256 * (q + 1))
             for q in (2 * half, 2 * half + 1):
@@ -297,7 +299,7 @@ def tile_picked_voxel_gelu_p_kernel(
         for half in range(2):
             for m in range(4):
                 i = 4 * half + m
-                if i in (2, 4, 6):
+                if i in (4, 5, 7):
                     nc.vector.tensor_copy(out=res[i][:], in_=accs[half, m][:])
                 else:
                     nc.scalar.copy(out=res[i][:], in_=accs[half, m][:])

@@ -53,8 +53,9 @@ def tile_picked_voxel_gelu_p_kernel(
         pieces = [(0, 128), (128, 128), (256, 128), (384, 128), (512, 512)]
         raw1 = {}
         for c0, wd in pieces:
-            for g in range(2):
+            for g in range(1 if c0 == 512 else 2):
                 raw1[c0, g] = sb("raw1_%d_%d" % (c0, g), [P, PACK, wd], F32)
+        late = [sb("late%d" % u, [P, PACK, 256], F32) for u in range(2)]
         raw2 = [sb("raw2_%d" % g, [P, PACK, N], F32) for g in range(2)]
 
         def load_w1(c0, wd, g):
@@ -81,9 +82,10 @@ def tile_picked_voxel_gelu_p_kernel(
         for c0, wd in pieces[1:4]:
             for g in range(2):
                 load_w1(c0, wd, g)
-        for g in range(2):
-            for c0, wd in pieces[4:]:
-                load_w1(c0, wd, g)
+        load_w1(512, 512, 0)
+        for u in range(2):
+            rows = w1[KP:, 512 + 256 * u : 512 + 256 * (u + 1)]
+            nc.sync.dma_start(out=late[u][:], in_=rows.rearrange("(p j) c -> p j c", j=PACK))
         for g in range(2):
             rows = w2[g * KP : (g + 1) * KP, :]
             nc.sync.dma_start(out=raw2[g][:], in_=rows.rearrange("(p j) n -> p j n", j=PACK))
@@ -125,10 +127,10 @@ def tile_picked_voxel_gelu_p_kernel(
                 g1a[c][:].rearrange("p g m j -> p (g m j)"),
             )
 
-        def cast_b(g, half):
+        def cast_b(g, m0, m1, src):
             nc.scalar.copy(
-                out=g1b[g][:, :, 64 * half : 64 * half + 64, :].rearrange("p t m j -> p m j t"),
-                in_=raw1[512, g][:, :, 256 * half : 256 * (half + 1)].rearrange("p j (m t) -> p m j t", t=PACK),
+                out=g1b[g][:, :, m0:m1, :].rearrange("p t m j -> p m j t"),
+                in_=src.rearrange("p j (m t) -> p m j t", t=PACK),
             )
 
         def quant_b(g):
@@ -201,9 +203,6 @@ def tile_picked_voxel_gelu_p_kernel(
                 out=dst.rearrange("p (v u) -> p v u", u=2), in_=src[:, :, lo:hi].rearrange("p u v -> p v u")
             )
 
-        def cast_w2(g, u, copy=nc.scalar.copy):
-            interleave(g2[g][:, 256 * u : 256 * (u + 1), :], raw2[g][:, :, 256 * u : 256 * (u + 1)], copy)
-
         def quant_z(g, lo, hi):
             quantize(cz[g][:, lo:hi], sz[g][:, lo:hi], gz[g][:, lo:hi, :].rearrange("p v j -> p (v j)"))
 
@@ -229,13 +228,17 @@ def tile_picked_voxel_gelu_p_kernel(
                 xw[g][:, lo:hi], xw_all[g][:].bitcast(U32).indirect(offs_sb[:, lo // 16 : hi // 16])
             )
 
+        def gather_scales(lo, hi):
+            nc.vector.tensor_copy(xs[:, lo:hi], xs_all[:].bitcast(U8).indirect(offs_sb[:, lo // 16 : hi // 16]))
+
         gather_words(0, 0, S)
-        nc.vector.tensor_copy(xs[:], xs_all[:].bitcast(U8).indirect(offs_sb[:]))
+        gather_scales(0, 256)
         for g in range(2):
             cast_a(0, g)
             quantize(c1a[0][:, g, :], s1a[0][:, g, :], g1a[0][:, g, :, :].rearrange("p m j -> p (m j)"))
         gather_words(1, 0, 256)
         gather_words(1, 256, S)
+        gather_scales(256, S)
         layer1(0, 0, 0, 256)
         scatter(0, 0, 256)
         cast_a(1, 0)
@@ -250,11 +253,12 @@ def tile_picked_voxel_gelu_p_kernel(
             layer1(c - 1, c % 2, 0, S, "raw1_%d_1" % (c * P))
             turn(c - 2)
             scatter(c - 1, 0, S)
-        for g in range(2):
-            cast_b(g, 0)
-            cast_b(g, 1)
-            quant_b(g)
-        layer1(3, 0, 0, S, "raw1_512_1")
+        cast_b(0, 0, P, raw1[512, 0][:])
+        quant_b(0)
+        for u in range(2):
+            cast_b(1, 64 * u, 64 * (u + 1), late[u][:])
+        quant_b(1)
+        layer1(3, 0, 0, S, "late1")
         turn(2, (0,))
         scatter(3, 0, S)
         zt = sb("zt", [P, 8, KP], BF16, "g1b_1")
@@ -267,15 +271,13 @@ def tile_picked_voxel_gelu_p_kernel(
         turn(3)
         scatter(4, 0, S)
         scatter(5, 0, S)
-        cast_w2(0, 0)
-        cast_w2(0, 1)
+        interleave(g2[0][:], raw2[0][:])
         pairs = sb("pairs", [P, 2, V, 2], BF16, "raw2_0")
         round_turned(3)
         layer1(6, 7, 0, S)
         round_pair(4, 0, V)
         scatter(6, 0, S)
-        cast_w2(1, 0)
-        cast_w2(1, 1)
+        interleave(g2[1][:], raw2[1][:], nc.vector.tensor_copy)
         for g in range(2):
             quantize(c2[g][:], s2[g][:], g2[g][:].rearrange("p n j -> p (n j)"))
         for half in range(2):
@@ -290,7 +292,7 @@ def tile_picked_voxel_gelu_p_kernel(
         layer2(0, 1)
         for half in range(2):
             for q in (2 * half, 2 * half + 1):
-                round_pair(7, 256 * q, 256 * (q + 1), nc.vector.tensor_copy)
+                round_pair(7, 256 * q, 256 * (q + 1), nc.scalar.copy if half else nc.vector.tensor_copy)
             for q in (2 * half, 2 * half + 1):
                 join_pairs(256 * q, 256 * (q + 1))
             for q in (2 * half, 2 * half + 1):

@@ -89,9 +89,9 @@ def tile_picked_voxel_gelu_p_kernel(
         for g in range(2):
             rows = w2[g * KP : (g + 1) * KP, :]
             nc.sync.dma_start(out=raw2[g][:], in_=rows.rearrange("(p j) n -> p j n", j=PACK))
-        nc.vector.memset(windows[0][:], 0.0)
-        for win in windows[1:]:
-            nc.gpsimd.memset(win[:], 0.0)
+        nc.gpsimd.memset(windows[2][:], 0.0)
+        for win in windows[:2]:
+            nc.vector.memset(win[:], 0.0)
         make_identity(nc, ident[:])
 
         def interleave(dst, src, copy=nc.scalar.copy):
@@ -115,7 +115,6 @@ def tile_picked_voxel_gelu_p_kernel(
         gz = [sb("gz%d" % g, [P, V, PACK], BF16) for g in range(2)]
         cz = [sb("cz%d" % g, [P, V], U32) for g in range(2)]
         sz = [sb("sz%d" % g, [P, V], U8) for g in range(2)]
-        res = [sb("res%d" % i, [P, BANK], F32) for i in range(8)]
 
         def cast_a(c, g):
             interleave(g1a[c][:, g, :, :], raw1[c * P, g][:])
@@ -208,20 +207,28 @@ def tile_picked_voxel_gelu_p_kernel(
 
         accs = {}
 
-        def layer2(g, half):
+        def layer2(g, lo, hi):
             for m in range(4):
                 if g == 0:
-                    accs[half, m] = bank(4 * half + m, [P, BANK])
-                cols = slice(half * BANK, (half + 1) * BANK)
+                    accs[lo, m] = bank(4 * (lo // BANK) + m, [P, hi - lo])
                 nc.tensor.matmul_mx(
-                    out=accs[half, m][:],
+                    out=accs[lo, m][:],
                     lhsT=c2[g][:, m * P : (m + 1) * P].bitcast(FP8X4),
                     lhsT_scale=s2[g][:, m * P : (m + 1) * P],
-                    rhs=cz[g][:, cols].bitcast(FP8X4),
-                    rhs_scale=sz[g][:, cols],
+                    rhs=cz[g][:, lo:hi].bitcast(FP8X4),
+                    rhs_scale=sz[g][:, lo:hi],
                     start=(g == 0),
                     stop=(g == 1),
                 )
+
+        def store(lo, hi):
+            for m in range(4):
+                res = sb("res%d_%d" % (lo, m), [P, hi - lo], F32)
+                if lo == BANK and m != 2:
+                    nc.vector.tensor_copy(out=res[:], in_=accs[lo, m][:])
+                else:
+                    nc.scalar.copy(out=res[:], in_=accs[lo, m][:])
+                nc.sync.dma_start(out=out[m * P : (m + 1) * P, lo:hi], in_=res[:])
 
         def gather_words(g, lo, hi):
             nc.vector.tensor_copy(
@@ -277,7 +284,8 @@ def tile_picked_voxel_gelu_p_kernel(
         layer1(6, 7, 0, S)
         round_pair(4, 0, V)
         scatter(6, 0, S)
-        interleave(g2[1][:], raw2[1][:], nc.vector.tensor_copy)
+        interleave(g2[1][:, :384, :], raw2[1][:, :, :384])
+        interleave(g2[1][:, 384:, :], raw2[1][:, :, 384:], nc.vector.tensor_copy)
         for g in range(2):
             quantize(c2[g][:], s2[g][:], g2[g][:].rearrange("p n j -> p (n j)"))
         for half in range(2):
@@ -288,21 +296,22 @@ def tile_picked_voxel_gelu_p_kernel(
             scatter(7, 256 * half, 256 * (half + 1))
         round_pair(5, 0, V)
         round_pair(6, 0, V)
-        layer2(0, 0)
-        layer2(0, 1)
-        for half in range(2):
-            for q in (2 * half, 2 * half + 1):
-                round_pair(7, 256 * q, 256 * (q + 1), nc.scalar.copy if half else nc.vector.tensor_copy)
-            for q in (2 * half, 2 * half + 1):
-                join_pairs(256 * q, 256 * (q + 1))
-            for q in (2 * half, 2 * half + 1):
-                quant_z(1, 256 * q, 256 * (q + 1))
-            layer2(1, half)
-        for half in range(2):
-            for m in range(4):
-                i = 4 * half + m
-                if i in (4, 5, 7):
-                    nc.vector.tensor_copy(out=res[i][:], in_=accs[half, m][:])
-                else:
-                    nc.scalar.copy(out=res[i][:], in_=accs[half, m][:])
-                nc.sync.dma_start(out=out[m * P : (m + 1) * P, half * BANK : (half + 1) * BANK], in_=res[i][:])
+        layer2(0, 0, 256)
+        layer2(0, BANK, V)
+        for q in range(4):
+            round_pair(7, 256 * q, 256 * (q + 1), nc.vector.tensor_copy if q < 2 else nc.scalar.copy)
+        join_pairs(0, 256)
+        join_pairs(256, BANK)
+        quant_z(1, 0, 256)
+        quant_z(1, 256, BANK)
+        join_pairs(BANK, 768)
+        join_pairs(768, V)
+        quant_z(1, BANK, 768)
+        quant_z(1, 768, V)
+        layer2(1, 0, 256)
+        store(0, 256)
+        layer2(0, 256, BANK)
+        layer2(1, 256, BANK)
+        store(256, BANK)
+        layer2(1, BANK, V)
+        store(BANK, V)

from contextlib import ExitStack

import concourse.mybir as mybir
from concourse.masks import make_identity

K, T, S, V, H, N = 1024, 1024, 512, 1024, 1024, 512
FLOPS = 2 * K * H * S + 2 * H * N * V

F32 = mybir.dt.float32
BF16 = mybir.dt.bfloat16
I32 = mybir.dt.int32
U32 = mybir.dt.uint32
U16 = mybir.dt.uint16
U8 = mybir.dt.uint8
FP8X4 = mybir.dt.float8_e4m3fn_x4
MULT = mybir.AluOpType.mult
GELU = mybir.ActivationFunctionType.Gelu_apprx_tanh

P = 128
PACK = 4
KP = P * PACK
BANK = 512
WINDOWS = 3
SLOT = {4: 2, 5: 0, 6: 1, 7: 3}


def tile_picked_voxel_gelu_p_kernel(
    tc, x_words, x_scales, w1, w2, gate, offs, pos1, out
):
    nc = tc.nc
    with ExitStack() as ctx:
        lists = ctx.enter_context(tc.tile_pool(name="lists", bufs=1))
        keep = ctx.enter_context(tc.tile_pool(name="keep", bufs=1))
        psum = ctx.enter_context(tc.psum_pool(name="psum", bufs=1))

        def sb(name, shape, dtype, tag=None):
            return keep.tile(shape, dtype, name=name, tag=tag or name, align_bytes=64)

        def bank(b, shape):
            return psum.tile(shape, F32, name="bank%d" % b)

        offs_sb = lists.tile([P, S // 16], U16, name="offs_sb")
        pos_sb = lists.tile([P, S // 16], U16, name="pos_sb")
        xs_all = sb("xs_all", [P, T // 4], I32)
        xw_all = [sb("xw_all%d" % g, [P, T], I32) for g in range(2)]
        xs = sb("xs", [P, S], U8)
        xw = [sb("xw%d" % g, [P, S], U32) for g in range(2)]
        gate_sb = sb("gate_sb", [P, S], F32)
        windows = [sb("window%d" % i, [P, V], F32) for i in range(WINDOWS)]
        ident = sb("ident", [P, P], F32)
        warm = sb("warm", [P, 8], F32)

        pieces = [(0, 128), (128, 128), (256, 128), (384, 128), (512, 512)]
        raw1 = {}
        for c0, wd in pieces:
            for g in range(1 if c0 == 512 else 2):
                raw1[c0, g] = sb("raw1_%d_%d" % (c0, g), [P, PACK, wd], F32)
        late = [sb("late%d" % u, [P, PACK, 256], F32) for u in range(2)]
        raw2 = [sb("raw2_%d" % g, [P, PACK, N], F32) for g in range(2)]

        def load_w1(c0, wd, g):
            rows = w1[g * KP : (g + 1) * KP, c0 : c0 + wd]
            nc.sync.dma_start(out=raw1[c0, g][:], in_=rows.rearrange("(p j) c -> p j c", j=PACK))

        def load_x(g):
            nc.sync.dma_start(out=xw_all[g][:], in_=x_words[g].rearrange("p c r -> p (c r)").bitcast(I32))

        nc.gpsimd.memset(xs_all[:], 0)
        nc.gpsimd.memset(warm[:], 0.0)
        nc.scalar.activation(out=warm[:, 4:5], in_=warm[:, 0:1], func=GELU)
        nc.sync.dma_start(offs_sb[:], offs)
        load_x(0)
        for q in range(4):
            nc.sync.dma_start(
                out=xs_all[32 * q : 32 * q + 8, :], in_=x_scales[:, 4 * q : 4 * q + 4, :].bitcast(I32)
            )
        load_w1(0, 128, 0)
        load_w1(0, 128, 1)
        load_x(1)
        nc.sync.dma_start(pos_sb[:], pos1)
        nc.sync.dma_start(out=gate_sb[:], in_=gate)
        for c0, wd in pieces[1:4]:
            for g in range(2):
                load_w1(c0, wd, g)
        load_w1(512, 512, 0)
        for u in range(2):
            rows = w1[KP:, 512 + 256 * u : 512 + 256 * (u + 1)]
            nc.sync.dma_start(out=late[u][:], in_=rows.rearrange("(p j) c -> p j c", j=PACK))
        for g in range(2):
            rows = w2[g * KP : (g + 1) * KP, :]
            nc.sync.dma_start(out=raw2[g][:], in_=rows.rearrange("(p j) n -> p j n", j=PACK))
        nc.gpsimd.memset(windows[2][:], 0.0)
        for win in windows[:2]:
            nc.vector.memset(win[:], 0.0)
        make_identity(nc, ident[:])

        def interleave(dst, src, copy=nc.scalar.copy):
            copy(
                out=dst.rearrange("p (c i) j -> p c j i", i=4), in_=src.rearrange("p j (c i) -> p c j i", i=4)
            )

        def quantize(codes, scales, grouped):
            nc.vector.quantize_mx(out=codes.bitcast(FP8X4), scales=scales, in_=grouped)

        g1a = [sb("g1a_%d" % c, [P, 2, P, PACK], BF16) for c in range(4)]
        c1a = [sb("c1a_%d" % c, [P, 2, P], U32) for c in range(4)]
        s1a = [sb("s1a_%d" % c, [P, 2, P], U8) for c in range(4)]
        g1b = [sb("g1b_%d" % g, [P, PACK, P, PACK], BF16) for g in range(2)]
        c1b = [sb("c1b_%d" % g, [P, PACK, P], U32) for g in range(2)]
        s1b = [sb("s1b_%d" % g, [P, PACK, P], U8) for g in range(2)]
        g2 = [sb("g2_%d" % g, [P, N, PACK], BF16) for g in range(2)]
        c2 = [sb("c2_%d" % g, [P, N], U32) for g in range(2)]
        s2 = [sb("s2_%d" % g, [P, N], U8) for g in range(2)]
        h = {}
        gz = [sb("gz%d" % g, [P, V, PACK], BF16) for g in range(2)]
        cz = [sb("cz%d" % g, [P, V], U32) for g in range(2)]
        sz = [sb("sz%d" % g, [P, V], U8) for g in range(2)]

        def cast_a(c, g):
            interleave(g1a[c][:, g, :, :], raw1[c * P, g][:])

        def quant_a(c):
            quantize(
                c1a[c][:].rearrange("p g m -> p (g m)"),
                s1a[c][:].rearrange("p g m -> p (g m)"),
                g1a[c][:].rearrange("p g m j -> p (g m j)"),
            )

        def cast_b(g, m0, m1, src):
            nc.scalar.copy(
                out=g1b[g][:, :, m0:m1, :].rearrange("p t m j -> p m j t"),
                in_=src.rearrange("p j (m t) -> p m j t", t=PACK),
            )

        def quant_b(g):
            quantize(
                c1b[g][:].rearrange("p t m -> p (t m)"),
                s1b[g][:].rearrange("p t m -> p (t m)"),
                g1b[g][:].rearrange("p t m j -> p (t m j)"),
            )

        def layer1(i, b, lo, hi, tag=None):
            acc = bank(b, [P, hi - lo])
            for g in range(2):
                if i < 4:
                    codes, scales = c1a[i][:, g, :], s1a[i][:, g, :]
                else:
                    codes, scales = c1b[g][:, SLOT[i], :], s1b[g][:, SLOT[i], :]
                nc.tensor.matmul_mx(
                    out=acc[:],
                    lhsT=codes.bitcast(FP8X4),
                    lhsT_scale=scales,
                    rhs=xw[g][:, lo:hi].bitcast(FP8X4),
                    rhs_scale=xs[4 * g :, lo:hi],
                    start=(g == 0),
                    stop=(g == 1),
                )
            h[i, hi] = sb("h%d_%d" % (i, lo), [P, hi - lo], F32, tag)
            nc.scalar.activation(out=h[i, hi][:], in_=acc[:], func=GELU)

        def scatter(i, lo, hi):
            nc.vector.tensor_tensor(
                windows[i % WINDOWS][:].indirect(pos_sb[:, lo // 16 : hi // 16]),
                h[i, hi][:],
                gate_sb[:, lo:hi],
                MULT,
            )

        turned = {}

        def turn(i, halves=(0, 1)):
            for half in halves:
                t = bank((2 + 2 * (i % 3)) % 6 + half, [P, 4, P])
                for b in range(4):
                    v0 = (4 * half + b) * P
                    nc.tensor.transpose(t[:, b, :], windows[i % WINDOWS][:, v0 : v0 + P], ident[:])
                turned[i, half] = t

        def round_turned(i):
            for half in range(2):
                nc.scalar.copy(out=zt[:, 4 * half : 4 * half + 4, i * P : (i + 1) * P], in_=turned[i, half][:])

        def turn_back(q):
            t = bank(4 + q, [P, 2, 2, P])
            for b in range(2):
                words = zt[:, 2 * q + b, :].bitcast(F32)
                for u in range(2):
                    nc.tensor.transpose(t[:, b, u, :], words[:, u : 2 * P : 2], ident[:])
            dst = gz[0][:, 256 * q : 256 * (q + 1), :].rearrange("p v j -> p (v j)").bitcast(F32)
            nc.scalar.copy(
                out=dst.rearrange("p (b v u) -> p b v u", b=2, u=2), in_=t[:].rearrange("p b u v -> p b v u")
            )

        def round_pair(i, lo, hi, copy=nc.scalar.copy):
            t = SLOT[i]
            copy(out=pairs[:, t // 2, lo:hi, t % 2], in_=windows[i % WINDOWS][:, lo:hi])

        def join_pairs(lo, hi):
            src = pairs[:].rearrange("p u v e -> p u (v e)").bitcast(F32)
            dst = gz[1][:, lo:hi, :].rearrange("p v j -> p (v j)").bitcast(F32)
            nc.vector.tensor_copy(
                out=dst.rearrange("p (v u) -> p v u", u=2), in_=src[:, :, lo:hi].rearrange("p u v -> p v u")
            )

        def quant_z(g, lo, hi):
            quantize(cz[g][:, lo:hi], sz[g][:, lo:hi], gz[g][:, lo:hi, :].rearrange("p v j -> p (v j)"))

        accs = {}

        def layer2(g, lo, hi):
            for m in range(4):
                if g == 0:
                    accs[lo, m] = bank(4 * (lo // BANK) + m, [P, hi - lo])
                nc.tensor.matmul_mx(
                    out=accs[lo, m][:],
                    lhsT=c2[g][:, m * P : (m + 1) * P].bitcast(FP8X4),
                    lhsT_scale=s2[g][:, m * P : (m + 1) * P],
                    rhs=cz[g][:, lo:hi].bitcast(FP8X4),
                    rhs_scale=sz[g][:, lo:hi],
                    start=(g == 0),
                    stop=(g == 1),
                )

        def store(lo, hi):
            for m in range(4):
                res = sb("res%d_%d" % (lo, m), [P, hi - lo], F32)
                if lo == BANK and m != 2:
                    nc.vector.tensor_copy(out=res[:], in_=accs[lo, m][:])
                else:
                    nc.scalar.copy(out=res[:], in_=accs[lo, m][:])
                nc.sync.dma_start(out=out[m * P : (m + 1) * P, lo:hi], in_=res[:])

        def gather_words(g, lo, hi):
            nc.vector.tensor_copy(
                xw[g][:, lo:hi], xw_all[g][:].bitcast(U32).indirect(offs_sb[:, lo // 16 : hi // 16])
            )

        def gather_scales(lo, hi):
            nc.vector.tensor_copy(xs[:, lo:hi], xs_all[:].bitcast(U8).indirect(offs_sb[:, lo // 16 : hi // 16]))

        gather_words(0, 0, S)
        gather_scales(0, 256)
        for g in range(2):
            cast_a(0, g)
            quantize(c1a[0][:, g, :], s1a[0][:, g, :], g1a[0][:, g, :, :].rearrange("p m j -> p (m j)"))
        gather_words(1, 0, 256)
        gather_words(1, 256, S)
        gather_scales(256, S)
        layer1(0, 0, 0, 256)
        scatter(0, 0, 256)
        cast_a(1, 0)
        cast_a(1, 1)
        quant_a(1)
        layer1(0, 1, 256, S, "raw1_128_1")
        scatter(0, 256, S)
        for c in range(2, 4):
            cast_a(c, 0)
            cast_a(c, 1)
            quant_a(c)
            layer1(c - 1, c % 2, 0, S, "raw1_%d_1" % (c * P))
            turn(c - 2)
            scatter(c - 1, 0, S)
        cast_b(0, 0, P, raw1[512, 0][:])
        quant_b(0)
        for u in range(2):
            cast_b(1, 64 * u, 64 * (u + 1), late[u][:])
        quant_b(1)
        layer1(3, 0, 0, S, "late1")
        turn(2, (0,))
        scatter(3, 0, S)
        zt = sb("zt", [P, 8, KP], BF16, "g1b_1")
        layer1(4, 1, 0, S)
        turn(2, (1,))
        round_turned(0)
        round_turned(1)
        layer1(5, 6, 0, S)
        round_turned(2)
        turn(3)
        scatter(4, 0, S)
        scatter(5, 0, S)
        interleave(g2[0][:], raw2[0][:])
        pairs = sb("pairs", [P, 2, V, 2], BF16, "raw2_0")
        round_turned(3)
        layer1(6, 7, 0, S)
        round_pair(4, 0, V)
        scatter(6, 0, S)
        interleave(g2[1][:, :384, :], raw2[1][:, :, :384])
        interleave(g2[1][:, 384:, :], raw2[1][:, :, 384:], nc.vector.tensor_copy)
        for g in range(2):
            quantize(c2[g][:], s2[g][:], g2[g][:].rearrange("p n j -> p (n j)"))
        for half in range(2):
            turn_back(2 * half)
            turn_back(2 * half + 1)
            quant_z(0, half * BANK, (half + 1) * BANK)
            layer1(7, 4 + 2 * half, 256 * half, 256 * (half + 1))
            scatter(7, 256 * half, 256 * (half + 1))
        round_pair(5, 0, V)
        round_pair(6, 0, V)
        layer2(0, 0, 256)
        layer2(0, BANK, V)
        for q in range(4):
            round_pair(7, 256 * q, 256 * (q + 1), nc.vector.tensor_copy if q < 2 else nc.scalar.copy)
        join_pairs(0, 256)
        join_pairs(256, BANK)
        quant_z(1, 0, 256)
        quant_z(1, 256, BANK)
        join_pairs(BANK, 768)
        join_pairs(768, V)
        quant_z(1, BANK, 768)
        quant_z(1, 768, V)
        layer2(1, 0, 256)
        store(0, 256)
        layer2(0, 256, BANK)
        layer2(1, 256, BANK)
        store(256, BANK)
        layer2(1, BANK, V)
        store(BANK, V)
